import numpy as np
import ml_dtypes

BF16 = ml_dtypes.bfloat16


def bf(x):
    return np.asarray(x, np.float32).astype(BF16)


def f32(x):
    return np.asarray(x, np.float32)


def f64(x):
    return np.asarray(x).astype(np.float64)


def striped(idx):
    return np.tile(idx.reshape(-1, 16).T, (8, 1))


S, K, M, N = 512, 512, 512, 256


def setup_inputs():
    return {"base": bf(np.random.standard_normal((M, S))), "x": bf(np.random.standard_normal((K, N))), "w": bf(np.random.standard_normal((K, M)) / np.sqrt(K)), "c": f32(0.2 + 0.8 * np.random.random_sample((1, S))), "offs": striped(np.random.permutation(S)[:N])}


def reference(base, x, w, c, offs):
    idx = offs[:16].T.reshape(-1)
    z = f64(base).copy()
    z[:, idx] += f64(w).T @ f64(x)
    return z * f64(c)

@@ -1,0 +1,52 @@
+import concourse.mybir as mybir
+from concourse.masks import make_identity
+
+P = 128
+M, S, K, N = 512, 512, 512, 256
+M_BLOCKS = M // P
+K_BLOCKS = K // P
+FLOPS = 2 * K * M * N
+
+BF16, F32, U16 = mybir.dt.bfloat16, mybir.dt.float32, mybir.dt.uint16
+
+
+def tile_scatter_matmul_kernel(tc, base, x, w, c, offs, out):
+    nc = tc.nc
+    with (
+        tc.tile_pool(name="held", bufs=1) as held,
+        tc.tile_pool(name="results", bufs=M_BLOCKS) as results,
+        tc.psum_pool(name="banks", bufs=1) as banks,
+    ):
+        offsets = held.tile([P, N // 16], U16, name="offsets")
+        nc.sync.dma_start(offsets[:], offs)
+
+        ident = held.tile([P, P], BF16, name="ident")
+        make_identity(nc, ident[:])
+
+        base_rows = [held.tile([P, S], BF16, name=f"base_rows{mb}") for mb in range(M_BLOCKS)]
+        for mb in range(M_BLOCKS):
+            nc.sync.dma_start(base_rows[mb][:], base[mb * P : (mb + 1) * P, :])
+        x_rows = [held.tile([P, N], BF16, name=f"x_rows{kb}") for kb in range(K_BLOCKS)]
+        w_rows = [held.tile([P, M], BF16, name=f"w_rows{kb}") for kb in range(K_BLOCKS)]
+        for kb in range(K_BLOCKS):
+            nc.scalar.dma_start(x_rows[kb][:], x[kb * P : (kb + 1) * P, :])
+            nc.scalar.dma_start(w_rows[kb][:], w[kb * P : (kb + 1) * P, :])
+        factors = held.tile([P, S], F32, name="factors")
+        nc.gpsimd.dma_start(factors[:], c.partition_broadcast(P))
+
+        windows = [banks.tile([P, S], F32, name=f"window{mb}") for mb in range(M_BLOCKS)]
+        for mb in range(M_BLOCKS):
+            nc.tensor.matmul(windows[mb][:], ident[:], base_rows[mb][:], start=True, stop=False)
+
+        for mb in range(M_BLOCKS):
+            for kb in range(K_BLOCKS):
+                nc.tensor.matmul(
+                    windows[mb][:].indirect(offsets[:]),
+                    w_rows[kb][:, mb * P : (mb + 1) * P],
+                    x_rows[kb][:],
+                    start=False,
+                    stop=(kb == K_BLOCKS - 1),
+                )
+            scaled = results.tile([P, S], F32, name="scaled")
+            nc.vector.tensor_tensor(scaled[:], windows[mb][:], factors[:], mybir.AluOpType.mult)
+            nc.sync.dma_start(out[mb * P : (mb + 1) * P, :], scaled[:])

@@ -5,6 +5,7 @@ P = 128
 M, S, K, N = 512, 512, 512, 256
 M_BLOCKS = M // P
 K_BLOCKS = K // P
+WARM_MATMULS = 5
 FLOPS = 2 * K * M * N
 
 BF16, F32, U16 = mybir.dt.bfloat16, mybir.dt.float32, mybir.dt.uint16
@@ -19,6 +20,12 @@ def tile_scatter_matmul_kernel(tc, base, x, w, c, offs, out):
     ):
         offsets = held.tile([P, N // 16], U16, name="offsets")
         nc.sync.dma_start(offsets[:], offs)
+
+        zeros = held.tile([P, S], BF16, name="zeros")
+        nc.vector.memset(zeros[:], 0.0)
+        unread = banks.tile([P, S], F32, name="unread")
+        for i in range(WARM_MATMULS):
+            nc.tensor.matmul(unread[:], zeros[:, 0:P], zeros[:], start=True, stop=True)
 
         ident = held.tile([P, P], BF16, name="ident")
         make_identity(nc, ident[:])

@@ -5,7 +5,9 @@ P = 128
 M, S, K, N = 512, 512, 512, 256
 M_BLOCKS = M // P
 K_BLOCKS = K // P
-WARM_MATMULS = 5
+K_EARLY = K_BLOCKS // 2
+WARM_MATMULS = 3
+HALF = S // 2
 FLOPS = 2 * K * M * N
 
 BF16, F32, U16 = mybir.dt.bfloat16, mybir.dt.float32, mybir.dt.uint16
@@ -15,45 +17,56 @@ def tile_scatter_matmul_kernel(tc, base, x, w, c, offs, out):
     nc = tc.nc
     with (
         tc.tile_pool(name="held", bufs=1) as held,
-        tc.tile_pool(name="results", bufs=M_BLOCKS) as results,
+        tc.tile_pool(name="results", bufs=2 * M_BLOCKS) as results,
         tc.psum_pool(name="banks", bufs=1) as banks,
     ):
-        offsets = held.tile([P, N // 16], U16, name="offsets")
-        nc.sync.dma_start(offsets[:], offs)
-
         zeros = held.tile([P, S], BF16, name="zeros")
         nc.vector.memset(zeros[:], 0.0)
         unread = banks.tile([P, S], F32, name="unread")
         for i in range(WARM_MATMULS):
             nc.tensor.matmul(unread[:], zeros[:, 0:P], zeros[:], start=True, stop=True)
 
+        offsets = held.tile([P, N // 16], U16, name="offsets")
+        nc.sync.dma_start(offsets[:], offs)
+
         ident = held.tile([P, P], BF16, name="ident")
         make_identity(nc, ident[:])
 
         base_rows = [held.tile([P, S], BF16, name=f"base_rows{mb}") for mb in range(M_BLOCKS)]
-        for mb in range(M_BLOCKS):
-            nc.sync.dma_start(base_rows[mb][:], base[mb * P : (mb + 1) * P, :])
         x_rows = [held.tile([P, N], BF16, name=f"x_rows{kb}") for kb in range(K_BLOCKS)]
         w_rows = [held.tile([P, M], BF16, name=f"w_rows{kb}") for kb in range(K_BLOCKS)]
-        for kb in range(K_BLOCKS):
-            nc.scalar.dma_start(x_rows[kb][:], x[kb * P : (kb + 1) * P, :])
-            nc.scalar.dma_start(w_rows[kb][:], w[kb * P : (kb + 1) * P, :])
         factors = held.tile([P, S], F32, name="factors")
-        nc.gpsimd.dma_start(factors[:], c.partition_broadcast(P))
+        loads = [(base_rows[mb], base[mb * P : (mb + 1) * P, :]) for mb in range(M_BLOCKS)]
+        for kb in range(K_BLOCKS):
+            loads.append((x_rows[kb], x[kb * P : (kb + 1) * P, :]))
+            loads.append((w_rows[kb], w[kb * P : (kb + 1) * P, :]))
+        loads.append((factors, c.partition_broadcast(P)))
+        queues = [nc.scalar, nc.sync]
+        for i, (rows, source) in enumerate(loads):
+            queues[i % 2].dma_start(rows[:], source)
 
         windows = [banks.tile([P, S], F32, name=f"window{mb}") for mb in range(M_BLOCKS)]
         for mb in range(M_BLOCKS):
             nc.tensor.matmul(windows[mb][:], ident[:], base_rows[mb][:], start=True, stop=False)
 
+        def add_scattered(mb, kb):
+            nc.tensor.matmul(
+                windows[mb][:].indirect(offsets[:]),
+                w_rows[kb][:, mb * P : (mb + 1) * P],
+                x_rows[kb][:],
+                start=False,
+                stop=(kb == K_BLOCKS - 1),
+            )
+
+        for kb in range(K_EARLY):
+            for mb in range(M_BLOCKS):
+                add_scattered(mb, kb)
+
         for mb in range(M_BLOCKS):
-            for kb in range(K_BLOCKS):
-                nc.tensor.matmul(
-                    windows[mb][:].indirect(offsets[:]),
-                    w_rows[kb][:, mb * P : (mb + 1) * P],
-                    x_rows[kb][:],
-                    start=False,
-                    stop=(kb == K_BLOCKS - 1),
-                )
-            scaled = results.tile([P, S], F32, name="scaled")
-            nc.vector.tensor_tensor(scaled[:], windows[mb][:], factors[:], mybir.AluOpType.mult)
-            nc.sync.dma_start(out[mb * P : (mb + 1) * P, :], scaled[:])
+            for kb in range(K_EARLY, K_BLOCKS):
+                add_scattered(mb, kb)
+            for h in range(2):
+                cols = slice(h * HALF, (h + 1) * HALF)
+                scaled = results.tile([P, HALF], F32, name="scaled")
+                nc.vector.tensor_tensor(scaled[:], windows[mb][:, cols], factors[:, cols], mybir.AluOpType.mult)
+                queues[h].dma_start(out[mb * P : (mb + 1) * P, cols], scaled[:])

@@ -6,7 +6,6 @@ M, S, K, N = 512, 512, 512, 256
 M_BLOCKS = M // P
 K_BLOCKS = K // P
 K_EARLY = K_BLOCKS // 2
-WARM_MATMULS = 3
 HALF = S // 2
 FLOPS = 2 * K * M * N
 
@@ -20,12 +19,6 @@ def tile_scatter_matmul_kernel(tc, base, x, w, c, offs, out):
         tc.tile_pool(name="results", bufs=2 * M_BLOCKS) as results,
         tc.psum_pool(name="banks", bufs=1) as banks,
     ):
-        zeros = held.tile([P, S], BF16, name="zeros")
-        nc.vector.memset(zeros[:], 0.0)
-        unread = banks.tile([P, S], F32, name="unread")
-        for i in range(WARM_MATMULS):
-            nc.tensor.matmul(unread[:], zeros[:, 0:P], zeros[:], start=True, stop=True)
-
         offsets = held.tile([P, N // 16], U16, name="offsets")
         nc.sync.dma_start(offsets[:], offs)
 

@@ -19,24 +19,21 @@ def tile_scatter_matmul_kernel(tc, base, x, w, c, offs, out):
         tc.tile_pool(name="results", bufs=2 * M_BLOCKS) as results,
         tc.psum_pool(name="banks", bufs=1) as banks,
     ):
-        offsets = held.tile([P, N // 16], U16, name="offsets")
-        nc.sync.dma_start(offsets[:], offs)
-
         ident = held.tile([P, P], BF16, name="ident")
         make_identity(nc, ident[:])
 
         base_rows = [held.tile([P, S], BF16, name=f"base_rows{mb}") for mb in range(M_BLOCKS)]
+        for mb in range(M_BLOCKS):
+            nc.sync.dma_start(base_rows[mb][:], base[mb * P : (mb + 1) * P, :])
+        offsets = held.tile([P, N // 16], U16, name="offsets")
+        nc.sync.dma_start(offsets[:], offs)
         x_rows = [held.tile([P, N], BF16, name=f"x_rows{kb}") for kb in range(K_BLOCKS)]
         w_rows = [held.tile([P, M], BF16, name=f"w_rows{kb}") for kb in range(K_BLOCKS)]
-        factors = held.tile([P, S], F32, name="factors")
-        loads = [(base_rows[mb], base[mb * P : (mb + 1) * P, :]) for mb in range(M_BLOCKS)]
         for kb in range(K_BLOCKS):
-            loads.append((x_rows[kb], x[kb * P : (kb + 1) * P, :]))
-            loads.append((w_rows[kb], w[kb * P : (kb + 1) * P, :]))
-        loads.append((factors, c.partition_broadcast(P)))
-        queues = [nc.scalar, nc.sync]
-        for i, (rows, source) in enumerate(loads):
-            queues[i % 2].dma_start(rows[:], source)
+            nc.sync.dma_start(x_rows[kb][:], x[kb * P : (kb + 1) * P, :])
+            nc.sync.dma_start(w_rows[kb][:], w[kb * P : (kb + 1) * P, :])
+        factors = held.tile([P, S], F32, name="factors")
+        nc.sync.dma_start(factors[:], c.partition_broadcast(P))
 
         windows = [banks.tile([P, S], F32, name=f"window{mb}") for mb in range(M_BLOCKS)]
         for mb in range(M_BLOCKS):
@@ -55,6 +52,7 @@ def tile_scatter_matmul_kernel(tc, base, x, w, c, offs, out):
             for mb in range(M_BLOCKS):
                 add_scattered(mb, kb)
 
+        store_queues = [nc.scalar, nc.sync]
         for mb in range(M_BLOCKS):
             for kb in range(K_EARLY, K_BLOCKS):
                 add_scattered(mb, kb)
@@ -62,4 +60,4 @@ def tile_scatter_matmul_kernel(tc, base, x, w, c, offs, out):
                 cols = slice(h * HALF, (h + 1) * HALF)
                 scaled = results.tile([P, HALF], F32, name="scaled")
                 nc.vector.tensor_tensor(scaled[:], windows[mb][:, cols], factors[:, cols], mybir.AluOpType.mult)
-                queues[h].dma_start(out[mb * P : (mb + 1) * P, cols], scaled[:])
+                store_queues[h].dma_start(out[mb * P : (mb + 1) * P, cols], scaled[:])

@@ -27,11 +27,14 @@ def tile_scatter_matmul_kernel(tc, base, x, w, c, offs, out):
             nc.sync.dma_start(base_rows[mb][:], base[mb * P : (mb + 1) * P, :])
         offsets = held.tile([P, N // 16], U16, name="offsets")
         nc.sync.dma_start(offsets[:], offs)
-        x_rows = [held.tile([P, N], BF16, name=f"x_rows{kb}") for kb in range(K_BLOCKS)]
-        w_rows = [held.tile([P, M], BF16, name=f"w_rows{kb}") for kb in range(K_BLOCKS)]
-        for kb in range(K_BLOCKS):
-            nc.sync.dma_start(x_rows[kb][:], x[kb * P : (kb + 1) * P, :])
-            nc.sync.dma_start(w_rows[kb][:], w[kb * P : (kb + 1) * P, :])
+        x_by_block = x.rearrange("(p kb) n -> p kb n", kb=K_BLOCKS)
+        w_by_block = w.rearrange("(p kb) m -> p kb m", kb=K_BLOCKS)
+        x_rows, w_rows = [], []
+        for first in range(0, K_BLOCKS, K_EARLY):
+            x_rows.append(held.tile([P, K_EARLY, N], BF16, name=f"x_rows{first}"))
+            nc.sync.dma_start(x_rows[-1][:], x_by_block[:, first : first + K_EARLY, :])
+            w_rows.append(held.tile([P, K_EARLY, M], BF16, name=f"w_rows{first}"))
+            nc.sync.dma_start(w_rows[-1][:], w_by_block[:, first : first + K_EARLY, :])
         factors = held.tile([P, S], F32, name="factors")
         nc.sync.dma_start(factors[:], c.partition_broadcast(P))
 
@@ -40,10 +43,11 @@ def tile_scatter_matmul_kernel(tc, base, x, w, c, offs, out):
             nc.tensor.matmul(windows[mb][:], ident[:], base_rows[mb][:], start=True, stop=False)
 
         def add_scattered(mb, kb):
+            load, row = divmod(kb, K_EARLY)
             nc.tensor.matmul(
                 windows[mb][:].indirect(offsets[:]),
-                w_rows[kb][:, mb * P : (mb + 1) * P],
-                x_rows[kb][:],
+                w_rows[load][:, row, mb * P : (mb + 1) * P],
+                x_rows[load][:, row, :],
                 start=False,
                 stop=(kb == K_BLOCKS - 1),
             )

@@ -5,7 +5,6 @@ P = 128
 M, S, K, N = 512, 512, 512, 256
 M_BLOCKS = M // P
 K_BLOCKS = K // P
-K_EARLY = K_BLOCKS // 2
 HALF = S // 2
 FLOPS = 2 * K * M * N
 
@@ -27,14 +26,10 @@ def tile_scatter_matmul_kernel(tc, base, x, w, c, offs, out):
             nc.sync.dma_start(base_rows[mb][:], base[mb * P : (mb + 1) * P, :])
         offsets = held.tile([P, N // 16], U16, name="offsets")
         nc.sync.dma_start(offsets[:], offs)
-        x_by_block = x.rearrange("(p kb) n -> p kb n", kb=K_BLOCKS)
-        w_by_block = w.rearrange("(p kb) m -> p kb m", kb=K_BLOCKS)
-        x_rows, w_rows = [], []
-        for first in range(0, K_BLOCKS, K_EARLY):
-            x_rows.append(held.tile([P, K_EARLY, N], BF16, name=f"x_rows{first}"))
-            nc.sync.dma_start(x_rows[-1][:], x_by_block[:, first : first + K_EARLY, :])
-            w_rows.append(held.tile([P, K_EARLY, M], BF16, name=f"w_rows{first}"))
-            nc.sync.dma_start(w_rows[-1][:], w_by_block[:, first : first + K_EARLY, :])
+        x_rows = held.tile([P, K_BLOCKS, N], BF16, name="x_rows")
+        nc.sync.dma_start(x_rows[:], x.rearrange("(p kb) n -> p kb n", kb=K_BLOCKS))
+        w_rows = held.tile([P, K_BLOCKS, M], BF16, name="w_rows")
+        nc.sync.dma_start(w_rows[:], w.rearrange("(p kb) m -> p kb m", kb=K_BLOCKS))
         factors = held.tile([P, S], F32, name="factors")
         nc.sync.dma_start(factors[:], c.partition_broadcast(P))
 
@@ -42,24 +37,16 @@ def tile_scatter_matmul_kernel(tc, base, x, w, c, offs, out):
         for mb in range(M_BLOCKS):
             nc.tensor.matmul(windows[mb][:], ident[:], base_rows[mb][:], start=True, stop=False)
 
-        def add_scattered(mb, kb):
-            load, row = divmod(kb, K_EARLY)
-            nc.tensor.matmul(
-                windows[mb][:].indirect(offsets[:]),
-                w_rows[load][:, row, mb * P : (mb + 1) * P],
-                x_rows[load][:, row, :],
-                start=False,
-                stop=(kb == K_BLOCKS - 1),
-            )
-
-        for kb in range(K_EARLY):
-            for mb in range(M_BLOCKS):
-                add_scattered(mb, kb)
-
         store_queues = [nc.scalar, nc.sync]
         for mb in range(M_BLOCKS):
-            for kb in range(K_EARLY, K_BLOCKS):
-                add_scattered(mb, kb)
+            for kb in range(K_BLOCKS):
+                nc.tensor.matmul(
+                    windows[mb][:].indirect(offsets[:]),
+                    w_rows[:, kb, mb * P : (mb + 1) * P],
+                    x_rows[:, kb, :],
+                    start=False,
+                    stop=(kb == K_BLOCKS - 1),
+                )
             for h in range(2):
                 cols = slice(h * HALF, (h + 1) * HALF)
                 scaled = results.tile([P, HALF], F32, name="scaled")

@@ -4,7 +4,8 @@ from concourse.masks import make_identity
 P = 128
 M, S, K, N = 512, 512, 512, 256
 M_BLOCKS = M // P
-K_BLOCKS = K // P
+K_HALVES = 2
+K_PER_HALF = K // P // K_HALVES
 HALF = S // 2
 FLOPS = 2 * K * M * N
 
@@ -26,10 +27,12 @@ def tile_scatter_matmul_kernel(tc, base, x, w, c, offs, out):
             nc.sync.dma_start(base_rows[mb][:], base[mb * P : (mb + 1) * P, :])
         offsets = held.tile([P, N // 16], U16, name="offsets")
         nc.sync.dma_start(offsets[:], offs)
-        x_rows = held.tile([P, K_BLOCKS, N], BF16, name="x_rows")
-        nc.sync.dma_start(x_rows[:], x.rearrange("(p kb) n -> p kb n", kb=K_BLOCKS))
-        w_rows = held.tile([P, K_BLOCKS, M], BF16, name="w_rows")
-        nc.sync.dma_start(w_rows[:], w.rearrange("(p kb) m -> p kb m", kb=K_BLOCKS))
+        x_rows = [held.tile([P, K_PER_HALF, N], BF16, name=f"x_rows{h}") for h in range(K_HALVES)]
+        w_rows = [held.tile([P, K_PER_HALF, M], BF16, name=f"w_rows{h}") for h in range(K_HALVES)]
+        for h in range(K_HALVES):
+            rows = slice(h * K // K_HALVES, (h + 1) * K // K_HALVES)
+            nc.sync.dma_start(x_rows[h][:], x[rows, :].rearrange("(p r) n -> p r n", r=K_PER_HALF))
+            nc.sync.dma_start(w_rows[h][:], w[rows, :].rearrange("(p r) m -> p r m", r=K_PER_HALF))
         factors = held.tile([P, S], F32, name="factors")
         nc.sync.dma_start(factors[:], c.partition_broadcast(P))
 
@@ -37,18 +40,32 @@ def tile_scatter_matmul_kernel(tc, base, x, w, c, offs, out):
         for mb in range(M_BLOCKS):
             nc.tensor.matmul(windows[mb][:], ident[:], base_rows[mb][:], start=True, stop=False)
 
-        store_queues = [nc.scalar, nc.sync]
-        for mb in range(M_BLOCKS):
-            for kb in range(K_BLOCKS):
+        def add_half(mb, h):
+            for r in range(K_PER_HALF):
                 nc.tensor.matmul(
                     windows[mb][:].indirect(offsets[:]),
-                    w_rows[:, kb, mb * P : (mb + 1) * P],
-                    x_rows[:, kb, :],
+                    w_rows[h][:, r, mb * P : (mb + 1) * P],
+                    x_rows[h][:, r, :],
                     start=False,
-                    stop=(kb == K_BLOCKS - 1),
+                    stop=(h == K_HALVES - 1 and r == K_PER_HALF - 1),
                 )
-            for h in range(2):
-                cols = slice(h * HALF, (h + 1) * HALF)
+
+        store_queues = [nc.scalar, nc.sync]
+
+        def scale_and_store(mb):
+            for half in range(2):
+                cols = slice(half * HALF, (half + 1) * HALF)
                 scaled = results.tile([P, HALF], F32, name="scaled")
                 nc.vector.tensor_tensor(scaled[:], windows[mb][:, cols], factors[:, cols], mybir.AluOpType.mult)
-                store_queues[h].dma_start(out[mb * P : (mb + 1) * P, cols], scaled[:])
+                store_queues[half].dma_start(out[mb * P : (mb + 1) * P, cols], scaled[:])
+
+        add_half(0, 0)
+        add_half(1, 0)
+        add_half(0, 1)
+        scale_and_store(0)
+        add_half(1, 1)
+        scale_and_store(1)
+        for mb in range(2, M_BLOCKS):
+            add_half(mb, 0)
+            add_half(mb, 1)
+            scale_and_store(mb)

@@ -22,9 +22,11 @@ def tile_scatter_matmul_kernel(tc, base, x, w, c, offs, out):
         ident = held.tile([P, P], BF16, name="ident")
         make_identity(nc, ident[:])
 
-        base_rows = [held.tile([P, S], BF16, name=f"base_rows{mb}") for mb in range(M_BLOCKS)]
-        for mb in range(M_BLOCKS):
-            nc.sync.dma_start(base_rows[mb][:], base[mb * P : (mb + 1) * P, :])
+        base_rows = [held.tile([P, 2, S], BF16, name=f"base_rows{pair}") for pair in range(M_BLOCKS // 2)]
+        for pair in range(M_BLOCKS // 2):
+            nc.sync.dma_start(
+                base_rows[pair][:], base[pair * 2 * P : (pair + 1) * 2 * P, :].rearrange("(b p) s -> p b s", p=P)
+            )
         offsets = held.tile([P, N // 16], U16, name="offsets")
         nc.sync.dma_start(offsets[:], offs)
         x_rows = [held.tile([P, K_PER_HALF, N], BF16, name=f"x_rows{h}") for h in range(K_HALVES)]
@@ -38,7 +40,7 @@ def tile_scatter_matmul_kernel(tc, base, x, w, c, offs, out):
 
         windows = [banks.tile([P, S], F32, name=f"window{mb}") for mb in range(M_BLOCKS)]
         for mb in range(M_BLOCKS):
-            nc.tensor.matmul(windows[mb][:], ident[:], base_rows[mb][:], start=True, stop=False)
+            nc.tensor.matmul(windows[mb][:], ident[:], base_rows[mb // 2][:, mb % 2, :], start=True, stop=False)
 
         def add_half(mb, h):
             for r in range(K_PER_HALF):

@@ -7,6 +7,7 @@ M_BLOCKS = M // P
 K_HALVES = 2
 K_PER_HALF = K // P // K_HALVES
 HALF = S // 2
+WARM_UPS = 16
 FLOPS = 2 * K * M * N
 
 BF16, F32, U16 = mybir.dt.bfloat16, mybir.dt.float32, mybir.dt.uint16
@@ -19,6 +20,12 @@ def tile_scatter_matmul_kernel(tc, base, x, w, c, offs, out):
         tc.tile_pool(name="results", bufs=2 * M_BLOCKS) as results,
         tc.psum_pool(name="banks", bufs=1) as banks,
     ):
+        zeros = held.tile([P, P], BF16, name="zeros")
+        nc.gpsimd.memset(zeros[:], 0.0)
+        unread = banks.tile([P, P], F32, name="unread")
+        for i in range(WARM_UPS):
+            nc.tensor.matmul(unread[:], zeros[:], zeros[:], start=True, stop=True)
+
         ident = held.tile([P, P], BF16, name="ident")
         make_identity(nc, ident[:])
 

@@ -7,6 +7,8 @@ M_BLOCKS = M // P
 K_HALVES = 2
 K_PER_HALF = K // P // K_HALVES
 HALF = S // 2
+SQ = 32
+C_BLOCKS = S // SQ
 WARM_UPS = 16
 FLOPS = 2 * K * M * N
 
@@ -42,8 +44,18 @@ def tile_scatter_matmul_kernel(tc, base, x, w, c, offs, out):
             rows = slice(h * K // K_HALVES, (h + 1) * K // K_HALVES)
             nc.sync.dma_start(x_rows[h][:], x[rows, :].rearrange("(p r) n -> p r n", r=K_PER_HALF))
             nc.sync.dma_start(w_rows[h][:], w[rows, :].rearrange("(p r) m -> p r m", r=K_PER_HALF))
-        factors = held.tile([P, S], F32, name="factors")
-        nc.sync.dma_start(factors[:], c.partition_broadcast(P))
+        c_blocks = held.tile([P, SQ], F32, name="c_blocks", align_bytes=64)
+        nc.sync.dma_start(c_blocks[:], c.rearrange("o (b j) -> (o b) j", j=SQ).partition_broadcast(P // C_BLOCKS))
+
+        c_turned = held.tile([P, SQ], F32, name="c_turned", align_bytes=64)
+        nc.vector.transpose(c_turned[:], c_blocks[:])
+        c_repeated = held.tile([P, S], F32, name="c_repeated", align_bytes=64)
+        nc.vector.tensor_copy(
+            c_repeated[:].rearrange("p (b i) -> p b i", i=SQ),
+            c_turned[:, 0:C_BLOCKS].unsqueeze(2).to_broadcast([P, C_BLOCKS, SQ]),
+        )
+        factors = held.tile([P, S], F32, name="factors", align_bytes=64)
+        nc.vector.transpose(factors[:], c_repeated[:])
 
         windows = [banks.tile([P, S], F32, name=f"window{mb}") for mb in range(M_BLOCKS)]
         for mb in range(M_BLOCKS):

@@ -4,8 +4,7 @@ from concourse.masks import make_identity
 P = 128
 M, S, K, N = 512, 512, 512, 256
 M_BLOCKS = M // P
-K_HALVES = 2
-K_PER_HALF = K // P // K_HALVES
+PART_BLOCKS = (1, 3)
 HALF = S // 2
 SQ = 32
 C_BLOCKS = S // SQ
@@ -38,12 +37,13 @@ def tile_scatter_matmul_kernel(tc, base, x, w, c, offs, out):
             )
         offsets = held.tile([P, N // 16], U16, name="offsets")
         nc.sync.dma_start(offsets[:], offs)
-        x_rows = [held.tile([P, K_PER_HALF, N], BF16, name=f"x_rows{h}") for h in range(K_HALVES)]
-        w_rows = [held.tile([P, K_PER_HALF, M], BF16, name=f"w_rows{h}") for h in range(K_HALVES)]
-        for h in range(K_HALVES):
-            rows = slice(h * K // K_HALVES, (h + 1) * K // K_HALVES)
-            nc.sync.dma_start(x_rows[h][:], x[rows, :].rearrange("(p r) n -> p r n", r=K_PER_HALF))
-            nc.sync.dma_start(w_rows[h][:], w[rows, :].rearrange("(p r) m -> p r m", r=K_PER_HALF))
+        x_rows = [held.tile([P, blocks, N], BF16, name=f"x_rows{part}") for part, blocks in enumerate(PART_BLOCKS)]
+        w_rows = [held.tile([P, blocks, M], BF16, name=f"w_rows{part}") for part, blocks in enumerate(PART_BLOCKS)]
+        for part, blocks in enumerate(PART_BLOCKS):
+            first_row = sum(PART_BLOCKS[:part]) * P
+            rows = slice(first_row, first_row + blocks * P)
+            nc.sync.dma_start(x_rows[part][:], x[rows, :].rearrange("(p r) n -> p r n", r=blocks))
+            nc.sync.dma_start(w_rows[part][:], w[rows, :].rearrange("(p r) m -> p r m", r=blocks))
         c_blocks = held.tile([P, SQ], F32, name="c_blocks", align_bytes=64)
         nc.sync.dma_start(c_blocks[:], c.rearrange("o (b j) -> (o b) j", j=SQ).partition_broadcast(P // C_BLOCKS))
 
@@ -61,14 +61,14 @@ def tile_scatter_matmul_kernel(tc, base, x, w, c, offs, out):
         for mb in range(M_BLOCKS):
             nc.tensor.matmul(windows[mb][:], ident[:], base_rows[mb // 2][:, mb % 2, :], start=True, stop=False)
 
-        def add_half(mb, h):
-            for r in range(K_PER_HALF):
+        def add_part(mb, part):
+            for r in range(PART_BLOCKS[part]):
                 nc.tensor.matmul(
                     windows[mb][:].indirect(offsets[:]),
-                    w_rows[h][:, r, mb * P : (mb + 1) * P],
-                    x_rows[h][:, r, :],
+                    w_rows[part][:, r, mb * P : (mb + 1) * P],
+                    x_rows[part][:, r, :],
                     start=False,
-                    stop=(h == K_HALVES - 1 and r == K_PER_HALF - 1),
+                    stop=(part == 1 and r == PART_BLOCKS[part] - 1),
                 )
 
         store_queues = [nc.scalar, nc.sync]
@@ -80,13 +80,8 @@ def tile_scatter_matmul_kernel(tc, base, x, w, c, offs, out):
                 nc.vector.tensor_tensor(scaled[:], windows[mb][:, cols], factors[:, cols], mybir.AluOpType.mult)
                 store_queues[half].dma_start(out[mb * P : (mb + 1) * P, cols], scaled[:])
 
-        add_half(0, 0)
-        add_half(1, 0)
-        add_half(0, 1)
-        scale_and_store(0)
-        add_half(1, 1)
-        scale_and_store(1)
-        for mb in range(2, M_BLOCKS):
-            add_half(mb, 0)
-            add_half(mb, 1)
+        for mb in range(M_BLOCKS):
+            add_part(mb, 0)
+        for mb in range(M_BLOCKS):
+            add_part(mb, 1)
             scale_and_store(mb)

@@ -5,7 +5,7 @@ P = 128
 M, S, K, N = 512, 512, 512, 256
 M_BLOCKS = M // P
 PART_BLOCKS = (1, 3)
-HALF = S // 2
+W_LOADS = (1, 2)
 SQ = 32
 C_BLOCKS = S // SQ
 WARM_UPS = 16
@@ -18,7 +18,7 @@ def tile_scatter_matmul_kernel(tc, base, x, w, c, offs, out):
     nc = tc.nc
     with (
         tc.tile_pool(name="held", bufs=1) as held,
-        tc.tile_pool(name="results", bufs=2 * M_BLOCKS) as results,
+        tc.tile_pool(name="results", bufs=1) as results,
         tc.psum_pool(name="banks", bufs=1) as banks,
     ):
         zeros = held.tile([P, P], BF16, name="zeros")
@@ -38,14 +38,24 @@ def tile_scatter_matmul_kernel(tc, base, x, w, c, offs, out):
         offsets = held.tile([P, N // 16], U16, name="offsets")
         nc.sync.dma_start(offsets[:], offs)
         x_rows = [held.tile([P, blocks, N], BF16, name=f"x_rows{part}") for part, blocks in enumerate(PART_BLOCKS)]
-        w_rows = [held.tile([P, blocks, M], BF16, name=f"w_rows{part}") for part, blocks in enumerate(PART_BLOCKS)]
+        w_rows = [
+            [held.tile([P, blocks, M // W_LOADS[part]], BF16, name=f"w_rows{part}_{i}") for i in range(W_LOADS[part])]
+            for part, blocks in enumerate(PART_BLOCKS)
+        ]
+        c_blocks = held.tile([P, SQ], F32, name="c_blocks", align_bytes=64)
         for part, blocks in enumerate(PART_BLOCKS):
             first_row = sum(PART_BLOCKS[:part]) * P
             rows = slice(first_row, first_row + blocks * P)
             nc.sync.dma_start(x_rows[part][:], x[rows, :].rearrange("(p r) n -> p r n", r=blocks))
-            nc.sync.dma_start(w_rows[part][:], w[rows, :].rearrange("(p r) m -> p r m", r=blocks))
-        c_blocks = held.tile([P, SQ], F32, name="c_blocks", align_bytes=64)
-        nc.sync.dma_start(c_blocks[:], c.rearrange("o (b j) -> (o b) j", j=SQ).partition_broadcast(P // C_BLOCKS))
+            width = M // W_LOADS[part]
+            for i in range(W_LOADS[part]):
+                nc.sync.dma_start(
+                    w_rows[part][i][:], w[rows, i * width : (i + 1) * width].rearrange("(p r) m -> p r m", r=blocks)
+                )
+            if part == 0:
+                nc.sync.dma_start(
+                    c_blocks[:], c.rearrange("o (b j) -> (o b) j", j=SQ).partition_broadcast(P // C_BLOCKS)
+                )
 
         c_turned = held.tile([P, SQ], F32, name="c_turned", align_bytes=64)
         nc.vector.transpose(c_turned[:], c_blocks[:])
@@ -62,26 +72,30 @@ def tile_scatter_matmul_kernel(tc, base, x, w, c, offs, out):
             nc.tensor.matmul(windows[mb][:], ident[:], base_rows[mb // 2][:, mb % 2, :], start=True, stop=False)
 
         def add_part(mb, part):
+            windows_a_load = M_BLOCKS // W_LOADS[part]
+            w_tile = w_rows[part][mb // windows_a_load]
+            first_col = (mb % windows_a_load) * P
             for r in range(PART_BLOCKS[part]):
                 nc.tensor.matmul(
                     windows[mb][:].indirect(offsets[:]),
-                    w_rows[part][:, r, mb * P : (mb + 1) * P],
+                    w_tile[:, r, first_col : first_col + P],
                     x_rows[part][:, r, :],
                     start=False,
                     stop=(part == 1 and r == PART_BLOCKS[part] - 1),
                 )
 
-        store_queues = [nc.scalar, nc.sync]
+        store_queues = [nc.sync, nc.scalar]
 
-        def scale_and_store(mb):
-            for half in range(2):
-                cols = slice(half * HALF, (half + 1) * HALF)
-                scaled = results.tile([P, HALF], F32, name="scaled")
+        def scale_and_store(mb, pieces):
+            width = S // pieces
+            for piece in range(pieces):
+                cols = slice(piece * width, (piece + 1) * width)
+                scaled = results.tile([P, width], F32, name=f"scaled{mb}_{piece}")
                 nc.vector.tensor_tensor(scaled[:], windows[mb][:, cols], factors[:, cols], mybir.AluOpType.mult)
-                store_queues[half].dma_start(out[mb * P : (mb + 1) * P, cols], scaled[:])
+                store_queues[(mb + piece) % 2].dma_start(out[mb * P : (mb + 1) * P, cols], scaled[:])
 
         for mb in range(M_BLOCKS):
             add_part(mb, 0)
         for mb in range(M_BLOCKS):
             add_part(mb, 1)
-            scale_and_store(mb)
+            scale_and_store(mb, pieces=2 if mb == M_BLOCKS - 1 else 1)

@@ -8,7 +8,7 @@ PART_BLOCKS = (1, 3)
 W_LOADS = (1, 2)
 SQ = 32
 C_BLOCKS = S // SQ
-WARM_UPS = 16
+WARM_UPS = 8
 FLOPS = 2 * K * M * N
 
 BF16, F32, U16 = mybir.dt.bfloat16, mybir.dt.float32, mybir.dt.uint16

import concourse.mybir as mybir
from concourse.masks import make_identity

P = 128
M, S, K, N = 512, 512, 512, 256
M_BLOCKS = M // P
PART_BLOCKS = (1, 3)
W_LOADS = (1, 2)
SQ = 32
C_BLOCKS = S // SQ
WARM_UPS = 8
FLOPS = 2 * K * M * N

BF16, F32, U16 = mybir.dt.bfloat16, mybir.dt.float32, mybir.dt.uint16


def tile_scatter_matmul_kernel(tc, base, x, w, c, offs, out):
    nc = tc.nc
    with (
        tc.tile_pool(name="held", bufs=1) as held,
        tc.tile_pool(name="results", bufs=1) as results,
        tc.psum_pool(name="banks", bufs=1) as banks,
    ):
        zeros = held.tile([P, P], BF16, name="zeros")
        nc.gpsimd.memset(zeros[:], 0.0)
        unread = banks.tile([P, P], F32, name="unread")
        for i in range(WARM_UPS):
            nc.tensor.matmul(unread[:], zeros[:], zeros[:], start=True, stop=True)

        ident = held.tile([P, P], BF16, name="ident")
        make_identity(nc, ident[:])

        base_rows = [held.tile([P, 2, S], BF16, name=f"base_rows{pair}") for pair in range(M_BLOCKS // 2)]
        for pair in range(M_BLOCKS // 2):
            nc.sync.dma_start(
                base_rows[pair][:], base[pair * 2 * P : (pair + 1) * 2 * P, :].rearrange("(b p) s -> p b s", p=P)
            )
        offsets = held.tile([P, N // 16], U16, name="offsets")
        nc.sync.dma_start(offsets[:], offs)
        x_rows = [held.tile([P, blocks, N], BF16, name=f"x_rows{part}") for part, blocks in enumerate(PART_BLOCKS)]
        w_rows = [
            [held.tile([P, blocks, M // W_LOADS[part]], BF16, name=f"w_rows{part}_{i}") for i in range(W_LOADS[part])]
            for part, blocks in enumerate(PART_BLOCKS)
        ]
        c_blocks = held.tile([P, SQ], F32, name="c_blocks", align_bytes=64)
        for part, blocks in enumerate(PART_BLOCKS):
            first_row = sum(PART_BLOCKS[:part]) * P
            rows = slice(first_row, first_row + blocks * P)
            nc.sync.dma_start(x_rows[part][:], x[rows, :].rearrange("(p r) n -> p r n", r=blocks))
            width = M // W_LOADS[part]
            for i in range(W_LOADS[part]):
                nc.sync.dma_start(
                    w_rows[part][i][:], w[rows, i * width : (i + 1) * width].rearrange("(p r) m -> p r m", r=blocks)
                )
            if part == 0:
                nc.sync.dma_start(
                    c_blocks[:], c.rearrange("o (b j) -> (o b) j", j=SQ).partition_broadcast(P // C_BLOCKS)
                )

        c_turned = held.tile([P, SQ], F32, name="c_turned", align_bytes=64)
        nc.vector.transpose(c_turned[:], c_blocks[:])
        c_repeated = held.tile([P, S], F32, name="c_repeated", align_bytes=64)
        nc.vector.tensor_copy(
            c_repeated[:].rearrange("p (b i) -> p b i", i=SQ),
            c_turned[:, 0:C_BLOCKS].unsqueeze(2).to_broadcast([P, C_BLOCKS, SQ]),
        )
        factors = held.tile([P, S], F32, name="factors", align_bytes=64)
        nc.vector.transpose(factors[:], c_repeated[:])

        windows = [banks.tile([P, S], F32, name=f"window{mb}") for mb in range(M_BLOCKS)]
        for mb in range(M_BLOCKS):
            nc.tensor.matmul(windows[mb][:], ident[:], base_rows[mb // 2][:, mb % 2, :], start=True, stop=False)

        def add_part(mb, part):
            windows_a_load = M_BLOCKS // W_LOADS[part]
            w_tile = w_rows[part][mb // windows_a_load]
            first_col = (mb % windows_a_load) * P
            for r in range(PART_BLOCKS[part]):
                nc.tensor.matmul(
                    windows[mb][:].indirect(offsets[:]),
                    w_tile[:, r, first_col : first_col + P],
                    x_rows[part][:, r, :],
                    start=False,
                    stop=(part == 1 and r == PART_BLOCKS[part] - 1),
                )

        store_queues = [nc.sync, nc.scalar]

        def scale_and_store(mb, pieces):
            width = S // pieces
            for piece in range(pieces):
                cols = slice(piece * width, (piece + 1) * width)
                scaled = results.tile([P, width], F32, name=f"scaled{mb}_{piece}")
                nc.vector.tensor_tensor(scaled[:], windows[mb][:, cols], factors[:, cols], mybir.AluOpType.mult)
                store_queues[(mb + piece) % 2].dma_start(out[mb * P : (mb + 1) * P, cols], scaled[:])

        for mb in range(M_BLOCKS):
            add_part(mb, 0)
        for mb in range(M_BLOCKS):
            add_part(mb, 1)
            scale_and_store(mb, pieces=2 if mb == M_BLOCKS - 1 else 1)
